import numpy as np
import ml_dtypes


def mxq(x, axis, fmt="e4m3"):
    dtype, down = {"e4m3": (ml_dtypes.float8_e4m3fn, 7), "e5m2": (ml_dtypes.float8_e5m2, 14)}[fmt]
    v = np.moveaxis(np.asarray(x, np.float32).astype(ml_dtypes.bfloat16).astype(np.float64), axis, -1)
    blocks = v.reshape(v.shape[:-1] + (-1, 32))
    amax = np.abs(blocks).max(-1, keepdims=True)
    byte = np.maximum(np.where(amax > 0, np.frexp(amax)[1] - 1 + 127, 0) - down, 1)
    scale = np.exp2(byte - 127.0)
    codes = (blocks / scale).astype(np.float32).astype(dtype).astype(np.float64)
    return np.moveaxis((codes * scale).reshape(v.shape), -1, axis)


WIDE = False


def mx_kscale(k):
    if not WIDE:
        return np.ones(k)
    levels = np.array([10, -10, 5, -5, 0])
    if k % 512:
        return np.exp2(np.random.permutation(np.resize(levels, k // 32))).repeat(32)
    a = np.empty((k // 512, 16))
    for p in range(k // 512):
        a[p, :8] = np.random.permutation(np.resize(levels, 8))
        for g in range(8):
            far = levels[np.abs(levels - a[p, g]) >= 10]
            a[p, g + 8] = far[np.random.randint(len(far))]
    return np.exp2(a.ravel()).repeat(32)


def f64(x):
    return np.asarray(x).astype(np.float64)


def striped(idx):
    return np.tile(np.asarray(idx).reshape(-1, 16).T, (8, 1)).astype(np.uint16)


def unstriped(offs):
    return offs[:16].T.reshape(-1).astype(np.int64)


E2M1 = np.array([0.0, 0.5, 1.0, 1.5, 2.0, 3.0, 4.0, 6.0, -0.0, -0.5, -1.0, -1.5, -2.0, -3.0, -4.0, -6.0])


def pack_weight(w, fmt):
    k, n = w.shape
    w = f64(np.asarray(w, np.float32).astype(ml_dtypes.bfloat16)).reshape(k // 32, 32, n)
    amax = np.abs(w).max(1)
    if fmt == "e4m3":
        byte = np.frexp(amax)[1] - 1 + 127 - 7
    else:
        mant, ex = np.frexp(amax / 6.0)
        byte = np.where(mant > 0.5, ex, ex - 1) + 127
    byte = np.clip(np.where(amax > 0, byte, 1), 1, 254)
    scaled = (w * np.exp2(127.0 - byte)[:, None, :]).reshape(k, n).astype(np.float32)
    by_word = np.ascontiguousarray(scaled.reshape(k // 512, 128, 4, n).transpose(0, 1, 3, 2))
    if fmt == "e4m3":
        words = by_word.astype(ml_dtypes.float8_e4m3fn).view(np.uint8)
    else:
        c = by_word.astype(ml_dtypes.float4_e2m1fn).view(np.uint8) & 0xF
        words = (c[..., 0::2] | (c[..., 1::2] << 4)).reshape(k // 512, 128, 2 * n)
    return np.ascontiguousarray(words), np.ascontiguousarray(byte.astype(np.uint8).reshape(k // 512, 16, n))


def unpack_weight(words, scales, fmt):
    g, _, n = scales.shape
    words = np.ascontiguousarray(words).reshape(g, 128, n, -1)
    if fmt == "e4m3":
        vals = words.view(ml_dtypes.float8_e4m3fn).astype(np.float64)
    else:
        nib = np.empty((g, 128, n, 4), np.uint8)
        nib[..., 0::2] = words & 0xF
        nib[..., 1::2] = words >> 4
        vals = E2M1[nib]
    vals = vals * np.repeat(np.exp2(scales.astype(np.float64) - 127.0), 8, axis=1)[..., None]
    return vals.transpose(0, 1, 3, 2).reshape(g * 512, n)


B, N, T, D, DV, NQ = 2, 512, 2048, 512, 256, 256
CAP = 2.0


def setup_inputs():
    n = np.random.standard_normal
    seg = T // B
    idx = np.concatenate([b * seg + np.random.permutation(seg)[:N] for b in range(B)])
    s = mx_kscale(D)[:, None]
    u = np.ones(T)
    u[idx] = mx_kscale(B * N)
    r = np.random.uniform(0.5, 2.0, T)
    k = n((D, T)) / s
    v = n((DV, T)) / (u * r)
    kp = pack_weight(k, "e4m3")
    return {
        "qT": (n((B, D, NQ)) * s * (0.80 / np.sqrt(D))).astype(np.float32),
        "k_words": kp[0],
        "k_scales": kp[1],
        "vT": v.astype(np.float32),
        "vs": np.tile(u * r, (128, 1)).astype(np.float32),
        "kb": np.tile(n(T), (128, 1)).astype(np.float32),
        "offs": striped(idx),
    }


def reference(qT, k_words, k_scales, vT, vs, kb, offs):
    idx = unstriped(offs)
    k = unpack_weight(k_words, k_scales, "e4m3")
    v = f64(vT)
    pick = lambda x: x[:, idx].reshape(x.shape[0], B, N).transpose(1, 0, 2)
    q = f64(qT)
    score = mxq(q, 1, "e4m3").transpose(0, 2, 1) @ pick(k)
    score = score + pick(f64(kb))[:, :1, :]
    score = CAP * np.tanh(score / CAP)
    p = np.square(np.maximum(score, 0.0))
    total = p.sum(-1, keepdims=True) + 1.0
    w = p * pick(f64(vs))[:, :1, :]
    y = mxq(w, 2, "e4m3") @ mxq(pick(v).transpose(0, 2, 1), 1, "e4m3")
    y = y / total
    return y

@@ -1,0 +1,270 @@
+from contextlib import ExitStack
+
+import concourse.mybir as mybir
+from concourse.masks import make_identity
+
+B, N, T, D, DV, NQ = 2, 512, 2048, 512, 256, 256
+FLOPS = 2 * B * NQ * N * (D + DV)
+
+F32 = mybir.dt.float32
+BF16 = mybir.dt.bfloat16
+I32 = mybir.dt.int32
+U32 = mybir.dt.uint32
+U16 = mybir.dt.uint16
+U8 = mybir.dt.uint8
+FP8X4 = mybir.dt.float8_e4m3fn_x4
+ALU = mybir.AluOpType
+ACT = mybir.ActivationFunctionType
+
+P = 128
+PACK = 4
+SEG = T // B
+ROW = P - 1
+QT = NQ // P
+COLS = N // 16
+
+
+def dealt(ap, run):
+    return ap.rearrange("p (t g r) -> p g t r", t=PACK, r=run)
+
+
+def tile_attend_rel2_cap_kb_segb2q256n512t2048_kernel(tc, qT, k_words, k_scales, vT, vs, kb, offs, out):
+    nc = tc.nc
+    with ExitStack() as ctx:
+        sb = ctx.enter_context(tc.tile_pool(name="sb", bufs=1))
+        mx = ctx.enter_context(tc.psum_pool(name="mx", bufs=4))
+        tp = ctx.enter_context(tc.psum_pool(name="tp", bufs=4))
+
+        offsets = sb.tile([P, B * COLS], U16, name="offsets")
+        nc.sync.dma_start(offsets[:], offs)
+
+        ks_pool = sb.tile([P, T], U8, name="ks_pool", align_bytes=64)
+        kb_pool = sb.tile([P, T], F32, name="kb_pool", align_bytes=64)
+        vs_pool = sb.tile([P, T], F32, name="vs_pool", align_bytes=64)
+        kw_pool = sb.tile([P, T], I32, name="kw_pool", align_bytes=64)
+        v_pool = sb.tile([P, T], I32, name="v_pool", align_bytes=64)
+        ident = sb.tile([P, P], F32, name="ident")
+        warm = sb.tile([P, 1], F32, name="warm")
+
+        nc.vector.memset(ks_pool[:].bitcast(I32), 0)
+        nc.vector.memset(kb_pool[0:ROW, 0:SEG], 0.0)
+        nc.gpsimd.memset(warm[:], 0.0)
+        nc.scalar.activation(warm[:], warm[:], ACT.Tanh)
+        make_identity(nc, ident[:])
+        nc.gpsimd.memset(kb_pool[0:ROW, SEG:T], 0.0)
+        nc.gpsimd.memset(vs_pool[0:ROW, :], 0.0)
+
+        nc.sync.dma_start(kb_pool[ROW:P, :], kb[0:1, :])
+        words = k_words[0].rearrange("p t r -> p (t r)")
+        v_rows = vT.rearrange("(p h) t -> p h t", h=2)
+        q_raw = [sb.tile([P, PACK, NQ], F32, name=f"q_raw{b}") for b in range(B)]
+        v_raw = [sb.tile([P, 2, 512], F32, name=f"v_raw{c}") for c in range(4)]
+
+        def load_keys(b):
+            nc.sync.dma_start(
+                kw_pool[:, b * SEG : (b + 1) * SEG],
+                words[:, b * SEG * PACK : (b + 1) * SEG * PACK].bitcast(I32),
+            )
+
+        def load_q(b):
+            nc.sync.dma_start(q_raw[b][:], qT[b].rearrange("(p j) q -> p j q", j=PACK))
+
+        def load_v(c):
+            nc.sync.dma_start(v_raw[c][:], v_rows[:, :, c * 512 : (c + 1) * 512])
+
+        load_keys(0)
+        for quad in range(4):
+            nc.sync.dma_start(
+                ks_pool[32 * quad : 32 * quad + 4, :].bitcast(I32),
+                k_scales[0, 4 * quad : 4 * quad + 4, :].bitcast(I32),
+            )
+        load_q(0)
+        load_keys(1)
+        load_v(0)
+        load_q(1)
+        load_v(1)
+        nc.sync.dma_start(vs_pool[ROW:P, :], vs[0:1, :])
+        load_v(2)
+        load_v(3)
+
+        def gather(pool, b, name, dtype):
+            got = sb.tile([P, N], dtype, name=f"{name}{b}", align_bytes=64)
+            window = pool[:, 0 : (b + 1) * SEG].bitcast(U32)
+            nc.vector.tensor_copy(
+                dealt(got[:].bitcast(U32), 8), window.indirect(offsets[:, b * COLS : (b + 1) * COLS])
+            )
+            return got
+
+        def turn(src):
+            bank = tp.tile([P, PACK, P], F32, tag="turn", name="turn")
+            for t in range(PACK):
+                nc.tensor.transpose(bank[:, t, :], src[:, t * P : (t + 1) * P].bitcast(F32), ident[:])
+            return bank
+
+        def token_column(pool, b, name, factor):
+            got = gather(pool, b, name, F32)
+            bank = turn(got)
+            col = sb.tile([P, PACK], F32, name=f"{name}col{b}")
+            nc.scalar.activation(col[:], bank[:, :, ROW], ACT.Copy, scale=factor)
+            return col
+
+        def quantize(src, name):
+            width = src.shape[1] // PACK
+            codes = sb.tile([P, width], U32, name=f"{name}_codes", align_bytes=64)
+            scales = sb.tile([P, width], U8, name=f"{name}_scales", align_bytes=64)
+            nc.vector.quantize_mx(out=codes[:].bitcast(FP8X4), scales=scales[:], in_=src)
+            return codes, scales
+
+        def cast_q(b):
+            q_bf = sb.tile([P, NQ * PACK], BF16, name=f"q_bf{b}", align_bytes=64)
+            nc.scalar.activation(
+                q_bf[:].rearrange("p (c i j) -> p c j i", i=4, j=PACK),
+                q_raw[b][:].rearrange("p j (c i) -> p c j i", i=4),
+                ACT.Copy,
+            )
+            return q_bf
+
+        def cast_v(c):
+            nc.scalar.activation(
+                v_pool[:, c * 512 : (c + 1) * 512].bitcast(BF16).rearrange("p (c h) -> p c h", h=2),
+                v_raw[c][:].rearrange("p h c -> p c h"),
+                ACT.Copy,
+            )
+
+        def scores(b, half_kb, q_bf, func):
+            keys = gather(kw_pool, b, "keys", I32)
+            ks_got = sb.tile([P, N], U8, name=f"ks_got{b}", align_bytes=64)
+            nc.vector.tensor_copy(
+                ks_got[:], ks_pool[:, 0 : (b + 1) * SEG].indirect(offsets[:, b * COLS : (b + 1) * COLS])
+            )
+            q_codes, q_scales = quantize(q_bf[:], f"q{b}")
+            ks = sb.tile([P, N], U8, name=f"ks{b}", align_bytes=64)
+            nc.vector.tensor_copy(
+                dealt(ks[:].bitcast(I32), 2),
+                ks_got[:].bitcast(I32).rearrange("p (g t r) -> p g t r", t=PACK, r=2),
+            )
+            banks = []
+            for u in range(2):
+                bank = mx.tile([P, 2, NQ], F32, tag="mx", name="mxbank")
+                banks.append(bank)
+                for s in range(2):
+                    t = 2 * u + s
+                    nc.tensor.matmul_mx(
+                        out=bank[:, s, :],
+                        lhsT=keys[:, t * P : (t + 1) * P].bitcast(FP8X4),
+                        lhsT_scale=ks[:, t * P : (t + 1) * P],
+                        rhs=q_codes[:].bitcast(FP8X4),
+                        rhs_scale=q_scales[:],
+                        start=True,
+                        stop=True,
+                    )
+            return banks
+
+        def biased(b, banks, half_kb, func):
+            first = sb.tile([P, PACK, NQ], F32, name=f"first{b}")
+            for t in range(PACK):
+                nc.scalar.activation(
+                    first[:, t, :], banks[t // 2][:, t % 2, :], func, bias=half_kb[:, t : t + 1], scale=0.5
+                )
+            return first
+
+        def flat(tile3):
+            return tile3[:].rearrange("p t q -> p (t q)")
+
+        def values(b):
+            got = gather(v_pool, b, "vals", I32)
+            bank = turn(got)
+            v_bf = sb.tile([P, DV * PACK], BF16, name=f"v_bf{b}", align_bytes=64)
+            nc.scalar.copy(
+                v_bf[:].rearrange("p (e t) -> p e t", t=PACK),
+                bank[:].rearrange("p t j -> p (t j)").bitcast(BF16).rearrange("p (t e) -> p e t", t=PACK),
+            )
+            return v_bf
+
+        def row_sums(b, p4):
+            sums = tp.tile([P, PACK, P], F32, tag="turn", name="turn")
+            for qt in range(QT):
+                for t in range(PACK):
+                    nc.tensor.matmul(
+                        sums[:, qt, :],
+                        p4[:, t, qt * P : (qt + 1) * P],
+                        ident[:],
+                        start=(t == 0),
+                        stop=(t == PACK - 1),
+                        is_transpose=True,
+                    )
+            denom = sb.tile([P, QT], F32, name=f"denom{b}")
+            spent = sb.tile([P, QT, P], F32, name=f"spent{b}")
+            for qt in range(QT):
+                nc.scalar.activation(
+                    spent[:, qt, :], sums[:, qt, :], ACT.Copy, bias=1.0 / P, scale=4.0,
+                    accum_out=denom[:, qt : qt + 1],
+                )
+            return denom
+
+        def invert(b, denom):
+            inv = sb.tile([P, QT], F32, name=f"inv{b}")
+            nc.vector.reciprocal(inv[:], denom[:])
+            return inv
+
+        def weights(b, p4, vs4, qt, width):
+            w_bf = sb.tile([P, width * PACK], BF16, name=f"w_bf{b}_{qt}", align_bytes=64)
+            nc.vector.tensor_tensor(
+                w_bf[:].rearrange("p (c i t) -> p c t i", i=4, t=PACK),
+                p4[:, :, qt * P : qt * P + width].rearrange("p t (c i) -> p c t i", i=4),
+                vs4[:].unsqueeze(1).unsqueeze(3).to_broadcast([P, width // 4, PACK, 4]),
+                ALU.mult,
+            )
+            return w_bf
+
+        def product(b, qt, w_codes, w_scales, v_codes, v_scales, inv):
+            bank = mx.tile([P, 2, DV], F32, tag="mx", name="mxbank")
+            nc.tensor.matmul_mx(
+                out=bank[:, 0, :],
+                lhsT=w_codes.bitcast(FP8X4),
+                lhsT_scale=w_scales,
+                rhs=v_codes[:].bitcast(FP8X4),
+                rhs_scale=v_scales[:],
+                start=True,
+                stop=True,
+            )
+            res = sb.tile([P, DV], F32, name=f"res{b}_{qt}")
+            nc.scalar.activation(res[:], bank[:, 0, :], ACT.Copy, scale=inv[:, qt : qt + 1])
+            nc.sync.dma_start(out[b, qt * P : (qt + 1) * P, :], res[:])
+
+        kb0 = token_column(kb_pool, 0, "kb", 0.5)
+        banks0 = scores(0, kb0, cast_q(0), ACT.Relu)
+        cast_v(0)
+        kb1 = token_column(kb_pool, 1, "kb", 0.5)
+        q1 = cast_q(1)
+        x0 = biased(0, banks0, kb0, ACT.Relu)
+        banks1 = scores(1, kb1, q1, ACT.Tanh)
+        cast_v(1)
+        t0 = sb.tile([P, PACK, NQ], F32, name="t0")
+        nc.scalar.activation(flat(t0), flat(x0), ACT.Tanh)
+        p0 = sb.tile([P, PACK, NQ], F32, name="p0")
+        nc.scalar.activation(flat(p0), flat(t0), ACT.Square)
+        vs0 = token_column(vs_pool, 0, "vs", 4.0)
+        vs1 = token_column(vs_pool, 1, "vs", 4.0)
+        cast_v(2)
+        cast_v(3)
+        t1 = biased(1, banks1, kb1, ACT.Tanh)
+        v0 = values(0)
+        den0 = row_sums(0, p0)
+        w0 = weights(0, p0, vs0, 0, NQ)
+        v1 = values(1)
+        w0_codes, w0_scales = quantize(w0[:], "w0")
+        p1 = sb.tile([P, PACK, NQ], F32, name="p1")
+        nc.vector.scalar_tensor_tensor(flat(p1), flat(t1), 0.0, flat(t1), ALU.max, ALU.mult)
+        v0_codes, v0_scales = quantize(v0[:], "v0")
+        inv0 = invert(0, den0)
+        den1 = row_sums(1, p1)
+        w1 = [weights(1, p1, vs1, qt, P) for qt in range(QT)]
+        for qt in range(QT):
+            cols = slice(qt * P, (qt + 1) * P)
+            product(0, qt, w0_codes[:, cols], w0_scales[:, cols], v0_codes, v0_scales, inv0)
+        v1_codes, v1_scales = quantize(v1[:], "v1")
+        inv1 = invert(1, den1)
+        for qt in range(QT):
+            codes, scales = quantize(w1[qt][:], f"w1_{qt}")
+            product(1, qt, codes[:], scales[:], v1_codes, v1_scales, inv1)

@@ -46,19 +46,18 @@ def tile_attend_rel2_cap_kb_segb2q256n512t2048_kernel(tc, qT, k_words, k_scales,
         ident = sb.tile([P, P], F32, name="ident")
         warm = sb.tile([P, 1], F32, name="warm")
 
-        nc.vector.memset(ks_pool[:].bitcast(I32), 0)
-        nc.vector.memset(kb_pool[0:ROW, 0:SEG], 0.0)
+        nc.gpsimd.memset(ks_pool[:].bitcast(I32), 0)
+        nc.vector.memset(kb_pool[0:ROW, :], 0.0)
         nc.gpsimd.memset(warm[:], 0.0)
         nc.scalar.activation(warm[:], warm[:], ACT.Tanh)
         make_identity(nc, ident[:])
-        nc.gpsimd.memset(kb_pool[0:ROW, SEG:T], 0.0)
         nc.gpsimd.memset(vs_pool[0:ROW, :], 0.0)
 
         nc.sync.dma_start(kb_pool[ROW:P, :], kb[0:1, :])
         words = k_words[0].rearrange("p t r -> p (t r)")
         v_rows = vT.rearrange("(p h) t -> p h t", h=2)
-        q_raw = [sb.tile([P, PACK, NQ], F32, name=f"q_raw{b}") for b in range(B)]
-        v_raw = [sb.tile([P, 2, 512], F32, name=f"v_raw{c}") for c in range(4)]
+        q_raw = [sb.tile([P, PACK, NQ], F32, name=f"q_raw{b}", tag=f"q_raw{b}", align_bytes=64) for b in range(B)]
+        v_raw = [sb.tile([P, 2, 512], F32, name=f"v_raw{c}", tag=f"v_raw{c}", align_bytes=64) for c in range(4)]
 
         def load_keys(b):
             nc.sync.dma_start(
@@ -79,49 +78,72 @@ def tile_attend_rel2_cap_kb_segb2q256n512t2048_kernel(tc, qT, k_words, k_scales,
                 k_scales[0, 4 * quad : 4 * quad + 4, :].bitcast(I32),
             )
         load_q(0)
-        load_keys(1)
         load_v(0)
+        load_keys(1)
         load_q(1)
         load_v(1)
         nc.sync.dma_start(vs_pool[ROW:P, :], vs[0:1, :])
         load_v(2)
         load_v(3)
 
-        def gather(pool, b, name, dtype):
-            got = sb.tile([P, N], dtype, name=f"{name}{b}", align_bytes=64)
+        def gather(pool, b, name, dtype, slot):
+            got = sb.tile([P, N], dtype, name=f"{name}{b}", tag=slot, align_bytes=64)
             window = pool[:, 0 : (b + 1) * SEG].bitcast(U32)
             nc.vector.tensor_copy(
                 dealt(got[:].bitcast(U32), 8), window.indirect(offsets[:, b * COLS : (b + 1) * COLS])
             )
             return got
 
-        def turn(src):
+        def turn(src, first, step):
             bank = tp.tile([P, PACK, P], F32, tag="turn", name="turn")
             for t in range(PACK):
-                nc.tensor.transpose(bank[:, t, :], src[:, t * P : (t + 1) * P].bitcast(F32), ident[:])
+                c0 = first + t * step
+                nc.tensor.transpose(bank[:, t, :], src[:, c0 : c0 + P].bitcast(F32), ident[:])
             return bank
 
-        def token_column(pool, b, name, factor):
-            got = gather(pool, b, name, F32)
-            bank = turn(got)
-            col = sb.tile([P, PACK], F32, name=f"{name}col{b}")
-            nc.scalar.activation(col[:], bank[:, :, ROW], ACT.Copy, scale=factor)
+        def token_columns(pool, name, factor, slot):
+            got = sb.tile([P, B * N], F32, name=f"{name}_got", align_bytes=64)
+            nc.vector.tensor_copy(dealt(got[:].bitcast(U32), 8), pool[:].bitcast(U32).indirect(offsets[:]))
+            cols = sb.tile([P, B, PACK], F32, name=f"{name}col", tag=slot, align_bytes=64)
+            for b in range(B):
+                bank = turn(got, b * P, B * P)
+                nc.scalar.activation(cols[:, b, :], bank[:, :, ROW], ACT.Copy, scale=factor)
+            return cols
+
+        def bias_column(b, slot):
+            got = gather(kb_pool, b, "kb_got", F32, slot)
+            bank = turn(got, 0, P)
+            col = sb.tile([P, PACK], F32, name=f"kbcol{b}", tag="kbcol", align_bytes=64)
+            nc.scalar.activation(col[:], bank[:, :, ROW], ACT.Copy, scale=0.5)
             return col
+
+        def key_scales(b, slot):
+            got = sb.tile([P, N], U8, name=f"ks_got{b}", tag=slot, align_bytes=64)
+            nc.vector.tensor_copy(
+                got[:], ks_pool[:, 0 : (b + 1) * SEG].indirect(offsets[:, b * COLS : (b + 1) * COLS])
+            )
+            ks = sb.tile([P, N], U8, name=f"ks{b}", align_bytes=64)
+            nc.vector.tensor_copy(
+                dealt(ks[:].bitcast(I32), 2),
+                got[:].bitcast(I32).rearrange("p (g t r) -> p g t r", t=PACK, r=2),
+            )
+            return ks
 
         def quantize(src, name):
             width = src.shape[1] // PACK
-            codes = sb.tile([P, width], U32, name=f"{name}_codes", align_bytes=64)
+            codes = sb.tile([P, width], U32, name=f"{name}_codes", tag=f"{name}_codes", align_bytes=64)
             scales = sb.tile([P, width], U8, name=f"{name}_scales", align_bytes=64)
             nc.vector.quantize_mx(out=codes[:].bitcast(FP8X4), scales=scales[:], in_=src)
             return codes, scales
 
-        def cast_q(b):
-            q_bf = sb.tile([P, NQ * PACK], BF16, name=f"q_bf{b}", align_bytes=64)
-            nc.scalar.activation(
-                q_bf[:].rearrange("p (c i j) -> p c j i", i=4, j=PACK),
-                q_raw[b][:].rearrange("p j (c i) -> p c j i", i=4),
-                ACT.Copy,
-            )
+        def cast_q(b, on_pool):
+            q_bf = sb.tile([P, NQ * PACK], BF16, name=f"q_bf{b}", tag=f"q_bf{b}", align_bytes=64)
+            dst = q_bf[:].rearrange("p (c i j) -> p c j i", i=4, j=PACK)
+            src = q_raw[b][:].rearrange("p j (c i) -> p c j i", i=4)
+            if on_pool:
+                nc.gpsimd.tensor_scalar(dst, src, 1.0, 0.0, ALU.mult, ALU.add)
+            else:
+                nc.scalar.activation(dst, src, ACT.Copy)
             return q_bf
 
         def cast_v(c):
@@ -131,18 +153,9 @@ def tile_attend_rel2_cap_kb_segb2q256n512t2048_kernel(tc, qT, k_words, k_scales,
                 ACT.Copy,
             )
 
-        def scores(b, half_kb, q_bf, func):
-            keys = gather(kw_pool, b, "keys", I32)
-            ks_got = sb.tile([P, N], U8, name=f"ks_got{b}", align_bytes=64)
-            nc.vector.tensor_copy(
-                ks_got[:], ks_pool[:, 0 : (b + 1) * SEG].indirect(offsets[:, b * COLS : (b + 1) * COLS])
-            )
+        def scores(b, ks, q_bf):
+            keys = gather(kw_pool, b, "keys", I32, f"keys{b}")
             q_codes, q_scales = quantize(q_bf[:], f"q{b}")
-            ks = sb.tile([P, N], U8, name=f"ks{b}", align_bytes=64)
-            nc.vector.tensor_copy(
-                dealt(ks[:].bitcast(I32), 2),
-                ks_got[:].bitcast(I32).rearrange("p (g t r) -> p g t r", t=PACK, r=2),
-            )
             banks = []
             for u in range(2):
                 bank = mx.tile([P, 2, NQ], F32, tag="mx", name="mxbank")
@@ -160,8 +173,8 @@ def tile_attend_rel2_cap_kb_segb2q256n512t2048_kernel(tc, qT, k_words, k_scales,
                     )
             return banks
 
-        def biased(b, banks, half_kb, func):
-            first = sb.tile([P, PACK, NQ], F32, name=f"first{b}")
+        def biased(b, banks, half_kb, func, slot):
+            first = sb.tile([P, PACK, NQ], F32, name=f"first{b}", tag=slot, align_bytes=64)
             for t in range(PACK):
                 nc.scalar.activation(
                     first[:, t, :], banks[t // 2][:, t % 2, :], func, bias=half_kb[:, t : t + 1], scale=0.5
@@ -172,52 +185,54 @@ def tile_attend_rel2_cap_kb_segb2q256n512t2048_kernel(tc, qT, k_words, k_scales,
             return tile3[:].rearrange("p t q -> p (t q)")
 
         def values(b):
-            got = gather(v_pool, b, "vals", I32)
-            bank = turn(got)
-            v_bf = sb.tile([P, DV * PACK], BF16, name=f"v_bf{b}", align_bytes=64)
+            got = gather(v_pool, b, "vals", I32, f"vals{b}")
+            return turn(got, 0, P)
+
+        def values_out(b, bank, slot):
+            v_bf = sb.tile([P, DV * PACK], BF16, name=f"v_bf{b}", tag=slot, align_bytes=64)
             nc.scalar.copy(
                 v_bf[:].rearrange("p (e t) -> p e t", t=PACK),
                 bank[:].rearrange("p t j -> p (t j)").bitcast(BF16).rearrange("p (t e) -> p e t", t=PACK),
             )
             return v_bf
 
-        def row_sums(b, p4):
+        def row_sum(b, p4, qt, denom, on_vector):
             sums = tp.tile([P, PACK, P], F32, tag="turn", name="turn")
-            for qt in range(QT):
-                for t in range(PACK):
-                    nc.tensor.matmul(
-                        sums[:, qt, :],
-                        p4[:, t, qt * P : (qt + 1) * P],
-                        ident[:],
-                        start=(t == 0),
-                        stop=(t == PACK - 1),
-                        is_transpose=True,
-                    )
-            denom = sb.tile([P, QT], F32, name=f"denom{b}")
-            spent = sb.tile([P, QT, P], F32, name=f"spent{b}")
-            for qt in range(QT):
-                nc.scalar.activation(
-                    spent[:, qt, :], sums[:, qt, :], ACT.Copy, bias=1.0 / P, scale=4.0,
-                    accum_out=denom[:, qt : qt + 1],
+            for t in range(PACK):
+                nc.tensor.matmul(
+                    sums[:, 0, :],
+                    p4[:, t, qt * P : (qt + 1) * P],
+                    ident[:],
+                    start=(t == 0),
+                    stop=(t == PACK - 1),
+                    is_transpose=True,
                 )
-            return denom
+            spent = sb.tile([P, P], F32, name=f"spent{b}_{qt}")
+            if on_vector:
+                nc.vector.tensor_scalar(
+                    spent[:], sums[:, 0, :], 4.0, 1.0, ALU.mult, ALU.add, accum_out=denom[:, qt : qt + 1]
+                )
+            else:
+                nc.scalar.activation(
+                    spent[:], sums[:, 0, :], ACT.Copy, bias=1.0 / P, scale=4.0, accum_out=denom[:, qt : qt + 1]
+                )
 
         def invert(b, denom):
             inv = sb.tile([P, QT], F32, name=f"inv{b}")
             nc.vector.reciprocal(inv[:], denom[:])
             return inv
 
-        def weights(b, p4, vs4, qt, width):
+        def weights(b, p4, vs4, qt, width, eng):
             w_bf = sb.tile([P, width * PACK], BF16, name=f"w_bf{b}_{qt}", align_bytes=64)
-            nc.vector.tensor_tensor(
+            eng.tensor_tensor(
                 w_bf[:].rearrange("p (c i t) -> p c t i", i=4, t=PACK),
                 p4[:, :, qt * P : qt * P + width].rearrange("p t (c i) -> p c t i", i=4),
-                vs4[:].unsqueeze(1).unsqueeze(3).to_broadcast([P, width // 4, PACK, 4]),
+                vs4[:, b, :].unsqueeze(1).unsqueeze(3).to_broadcast([P, width // 4, PACK, 4]),
                 ALU.mult,
             )
             return w_bf
 
-        def product(b, qt, w_codes, w_scales, v_codes, v_scales, inv):
+        def product(b, qt, w_codes, w_scales, v_codes, v_scales, inv, on_vector):
             bank = mx.tile([P, 2, DV], F32, tag="mx", name="mxbank")
             nc.tensor.matmul_mx(
                 out=bank[:, 0, :],
@@ -229,42 +244,54 @@ def tile_attend_rel2_cap_kb_segb2q256n512t2048_kernel(tc, qT, k_words, k_scales,
                 stop=True,
             )
             res = sb.tile([P, DV], F32, name=f"res{b}_{qt}")
-            nc.scalar.activation(res[:], bank[:, 0, :], ACT.Copy, scale=inv[:, qt : qt + 1])
+            if on_vector:
+                nc.vector.tensor_scalar(res[:], bank[:, 0, :], inv[:, qt : qt + 1], None, ALU.mult)
+            else:
+                nc.scalar.activation(res[:], bank[:, 0, :], ACT.Copy, scale=inv[:, qt : qt + 1])
             nc.sync.dma_start(out[b, qt * P : (qt + 1) * P, :], res[:])
 
-        kb0 = token_column(kb_pool, 0, "kb", 0.5)
-        banks0 = scores(0, kb0, cast_q(0), ACT.Relu)
+        den = [sb.tile([P, QT], F32, name=f"den{b}") for b in range(B)]
+        kb0 = bias_column(0, "kb_got0")
+        ks0 = key_scales(0, "ks_got0")
+        q0 = cast_q(0, False)
         cast_v(0)
-        kb1 = token_column(kb_pool, 1, "kb", 0.5)
-        q1 = cast_q(1)
-        x0 = biased(0, banks0, kb0, ACT.Relu)
-        banks1 = scores(1, kb1, q1, ACT.Tanh)
-        cast_v(1)
-        t0 = sb.tile([P, PACK, NQ], F32, name="t0")
+        banks0 = scores(0, ks0, q0)
+        x0 = biased(0, banks0, kb0, ACT.Relu, "v_raw0")
+        kb1 = bias_column(1, "q_bf0")
+        ks1 = key_scales(1, "q0_codes")
+        q1 = cast_q(1, False)
+        banks1 = scores(1, ks1, q1)
+        t0 = sb.tile([P, PACK, NQ], F32, name="t0", tag="q_raw1", align_bytes=64)
         nc.scalar.activation(flat(t0), flat(x0), ACT.Tanh)
-        p0 = sb.tile([P, PACK, NQ], F32, name="p0")
+        cast_v(1)
+        p0 = sb.tile([P, PACK, NQ], F32, name="p0", tag="v_raw1", align_bytes=64)
         nc.scalar.activation(flat(p0), flat(t0), ACT.Square)
-        vs0 = token_column(vs_pool, 0, "vs", 4.0)
-        vs1 = token_column(vs_pool, 1, "vs", 4.0)
         cast_v(2)
+        vs4 = token_columns(vs_pool, "vs", 4.0, "v_raw2")
         cast_v(3)
-        t1 = biased(1, banks1, kb1, ACT.Tanh)
-        v0 = values(0)
-        den0 = row_sums(0, p0)
-        w0 = weights(0, p0, vs0, 0, NQ)
-        v1 = values(1)
+        t1 = biased(1, banks1, kb1, ACT.Tanh, "v_raw3")
+        vb0 = values(0)
+        w0 = weights(0, p0, vs4, 0, NQ, nc.vector)
+        vb1 = values(1)
+        v0 = values_out(0, vb0, "kbcol")
+        for qt in range(QT):
+            row_sum(0, p0, qt, den[0], False)
+        v1 = values_out(1, vb1, "v_bf1")
         w0_codes, w0_scales = quantize(w0[:], "w0")
         p1 = sb.tile([P, PACK, NQ], F32, name="p1")
-        nc.vector.scalar_tensor_tensor(flat(p1), flat(t1), 0.0, flat(t1), ALU.max, ALU.mult)
-        v0_codes, v0_scales = quantize(v0[:], "v0")
-        inv0 = invert(0, den0)
-        den1 = row_sums(1, p1)
-        w1 = [weights(1, p1, vs1, qt, P) for qt in range(QT)]
         for qt in range(QT):
             cols = slice(qt * P, (qt + 1) * P)
-            product(0, qt, w0_codes[:, cols], w0_scales[:, cols], v0_codes, v0_scales, inv0)
+            nc.vector.scalar_tensor_tensor(p1[:, :, cols], t1[:, :, cols], 0.0, t1[:, :, cols], ALU.max, ALU.mult)
+        v0_codes, v0_scales = quantize(v0[:], "v0")
+        inv0 = invert(0, den[0])
+        for qt in range(QT):
+            row_sum(1, p1, qt, den[1], False)
+        w1 = [weights(1, p1, vs4, qt, P, nc.vector) for qt in range(QT)]
+        for qt in range(QT):
+            cols = slice(qt * P, (qt + 1) * P)
+            product(0, qt, w0_codes[:, cols], w0_scales[:, cols], v0_codes, v0_scales, inv0, False)
         v1_codes, v1_scales = quantize(v1[:], "v1")
-        inv1 = invert(1, den1)
+        inv1 = invert(1, den[1])
         for qt in range(QT):
             codes, scales = quantize(w1[qt][:], f"w1_{qt}")
-            product(1, qt, codes[:], scales[:], v1_codes, v1_scales, inv1)
+            product(1, qt, codes[:], scales[:], v1_codes, v1_scales, inv1, qt == 1)

@@ -32,8 +32,8 @@ def tile_attend_rel2_cap_kb_segb2q256n512t2048_kernel(tc, qT, k_words, k_scales,
     nc = tc.nc
     with ExitStack() as ctx:
         sb = ctx.enter_context(tc.tile_pool(name="sb", bufs=1))
-        mx = ctx.enter_context(tc.psum_pool(name="mx", bufs=4))
-        tp = ctx.enter_context(tc.psum_pool(name="tp", bufs=4))
+        stage = ctx.enter_context(tc.tile_pool(name="stage", bufs=1))
+        ps = ctx.enter_context(tc.psum_pool(name="ps", bufs=1))
 
         offsets = sb.tile([P, B * COLS], U16, name="offsets")
         nc.sync.dma_start(offsets[:], offs)
@@ -56,8 +56,13 @@ def tile_attend_rel2_cap_kb_segb2q256n512t2048_kernel(tc, qT, k_words, k_scales,
         nc.sync.dma_start(kb_pool[ROW:P, :], kb[0:1, :])
         words = k_words[0].rearrange("p t r -> p (t r)")
         v_rows = vT.rearrange("(p h) t -> p h t", h=2)
-        q_raw = [sb.tile([P, PACK, NQ], F32, name=f"q_raw{b}", tag=f"q_raw{b}", align_bytes=64) for b in range(B)]
-        v_raw = [sb.tile([P, 2, 512], F32, name=f"v_raw{c}", tag=f"v_raw{c}", align_bytes=64) for c in range(4)]
+        q_raw = [stage.tile([P, PACK, NQ], F32, name=f"q_raw{b}", offset=4096 * b, align_bytes=64) for b in range(B)]
+        v_raw = [stage.tile([P, 2, 512], F32, name=f"v_raw{c}", offset=8192 + 4096 * c, align_bytes=64) for c in range(4)]
+
+        def place(shape, dtype, name, slot):
+            if isinstance(slot, int):
+                return stage.tile(shape, dtype, name=name, offset=slot, align_bytes=64)
+            return sb.tile(shape, dtype, name=name, tag=slot, align_bytes=64)
 
         def load_keys(b):
             nc.sync.dma_start(
@@ -79,60 +84,53 @@ def tile_attend_rel2_cap_kb_segb2q256n512t2048_kernel(tc, qT, k_words, k_scales,
             )
         load_q(0)
         load_v(0)
-        load_keys(1)
         load_q(1)
-        load_v(1)
+        load_keys(1)
         nc.sync.dma_start(vs_pool[ROW:P, :], vs[0:1, :])
+        load_v(1)
         load_v(2)
         load_v(3)
 
         def gather(pool, b, name, dtype, slot):
-            got = sb.tile([P, N], dtype, name=f"{name}{b}", tag=slot, align_bytes=64)
+            got = place([P, N], dtype, f"{name}{b}", slot)
             window = pool[:, 0 : (b + 1) * SEG].bitcast(U32)
             nc.vector.tensor_copy(
                 dealt(got[:].bitcast(U32), 8), window.indirect(offsets[:, b * COLS : (b + 1) * COLS])
             )
             return got
 
-        def turn(src, first, step):
-            bank = tp.tile([P, PACK, P], F32, tag="turn", name="turn")
+        def turn(src, tag):
+            bank = ps.tile([P, PACK, P], F32, tag=tag, name="turn")
             for t in range(PACK):
-                c0 = first + t * step
-                nc.tensor.transpose(bank[:, t, :], src[:, c0 : c0 + P].bitcast(F32), ident[:])
+                nc.tensor.transpose(bank[:, t, :], src[:, t * P : (t + 1) * P].bitcast(F32), ident[:])
             return bank
 
-        def token_columns(pool, name, factor, slot):
-            got = sb.tile([P, B * N], F32, name=f"{name}_got", align_bytes=64)
-            nc.vector.tensor_copy(dealt(got[:].bitcast(U32), 8), pool[:].bitcast(U32).indirect(offsets[:]))
-            cols = sb.tile([P, B, PACK], F32, name=f"{name}col", tag=slot, align_bytes=64)
-            for b in range(B):
-                bank = turn(got, b * P, B * P)
-                nc.scalar.activation(cols[:, b, :], bank[:, :, ROW], ACT.Copy, scale=factor)
-            return cols
-
-        def bias_column(b, slot):
-            got = gather(kb_pool, b, "kb_got", F32, slot)
-            bank = turn(got, 0, P)
-            col = sb.tile([P, PACK], F32, name=f"kbcol{b}", tag="kbcol", align_bytes=64)
-            nc.scalar.activation(col[:], bank[:, :, ROW], ACT.Copy, scale=0.5)
+        def token_column(pool, name, b, factor, got_slot, col_slot):
+            got = gather(pool, b, f"{name}_got", F32, got_slot)
+            bank = turn(got, f"column{b}")
+            col = place([P, PACK], F32, f"{name}col{b}", col_slot)
+            nc.scalar.activation(col[:], bank[:, :, ROW], ACT.Copy, scale=factor)
             return col
 
-        def key_scales(b, slot):
+        def gather_scales(b, slot):
             got = sb.tile([P, N], U8, name=f"ks_got{b}", tag=slot, align_bytes=64)
             nc.vector.tensor_copy(
                 got[:], ks_pool[:, 0 : (b + 1) * SEG].indirect(offsets[:, b * COLS : (b + 1) * COLS])
             )
-            ks = sb.tile([P, N], U8, name=f"ks{b}", align_bytes=64)
+            return got
+
+        def deal_scales(b, got):
+            ks = place([P, N], U8, f"ks{b}", 4096 * b)
             nc.vector.tensor_copy(
                 dealt(ks[:].bitcast(I32), 2),
                 got[:].bitcast(I32).rearrange("p (g t r) -> p g t r", t=PACK, r=2),
             )
             return ks
 
-        def quantize(src, name):
+        def quantize(src, name, slot=None):
             width = src.shape[1] // PACK
             codes = sb.tile([P, width], U32, name=f"{name}_codes", tag=f"{name}_codes", align_bytes=64)
-            scales = sb.tile([P, width], U8, name=f"{name}_scales", align_bytes=64)
+            scales = place([P, width], U8, f"{name}_scales", slot or f"{name}_scales")
             nc.vector.quantize_mx(out=codes[:].bitcast(FP8X4), scales=scales[:], in_=src)
             return codes, scales
 
@@ -153,12 +151,13 @@ def tile_attend_rel2_cap_kb_segb2q256n512t2048_kernel(tc, qT, k_words, k_scales,
                 ACT.Copy,
             )
 
-        def scores(b, ks, q_bf):
+        def scores(b, ks_got, q_bf):
             keys = gather(kw_pool, b, "keys", I32, f"keys{b}")
             q_codes, q_scales = quantize(q_bf[:], f"q{b}")
+            ks = deal_scales(b, ks_got)
             banks = []
             for u in range(2):
-                bank = mx.tile([P, 2, NQ], F32, tag="mx", name="mxbank")
+                bank = ps.tile([P, 2, NQ], F32, tag=f"mx{b}{u}", name="scores")
                 banks.append(bank)
                 for s in range(2):
                     t = 2 * u + s
@@ -174,7 +173,7 @@ def tile_attend_rel2_cap_kb_segb2q256n512t2048_kernel(tc, qT, k_words, k_scales,
             return banks
 
         def biased(b, banks, half_kb, func, slot):
-            first = sb.tile([P, PACK, NQ], F32, name=f"first{b}", tag=slot, align_bytes=64)
+            first = place([P, PACK, NQ], F32, f"first{b}", slot)
             for t in range(PACK):
                 nc.scalar.activation(
                     first[:, t, :], banks[t // 2][:, t % 2, :], func, bias=half_kb[:, t : t + 1], scale=0.5
@@ -184,38 +183,35 @@ def tile_attend_rel2_cap_kb_segb2q256n512t2048_kernel(tc, qT, k_words, k_scales,
         def flat(tile3):
             return tile3[:].rearrange("p t q -> p (t q)")
 
-        def values(b):
-            got = gather(v_pool, b, "vals", I32, f"vals{b}")
-            return turn(got, 0, P)
+        def values(b, slot):
+            got = gather(v_pool, b, "vals", I32, slot)
+            return turn(got, f"value{b}")
 
         def values_out(b, bank, slot):
-            v_bf = sb.tile([P, DV * PACK], BF16, name=f"v_bf{b}", tag=slot, align_bytes=64)
+            v_bf = place([P, DV * PACK], BF16, f"v_bf{b}", slot)
             nc.scalar.copy(
                 v_bf[:].rearrange("p (e t) -> p e t", t=PACK),
                 bank[:].rearrange("p t j -> p (t j)").bitcast(BF16).rearrange("p (t e) -> p e t", t=PACK),
             )
             return v_bf
 
-        def row_sum(b, p4, qt, denom, on_vector):
-            sums = tp.tile([P, PACK, P], F32, tag="turn", name="turn")
+        def turn_and_add(p4, qt, dst):
             for t in range(PACK):
                 nc.tensor.matmul(
-                    sums[:, 0, :],
+                    dst,
                     p4[:, t, qt * P : (qt + 1) * P],
                     ident[:],
                     start=(t == 0),
                     stop=(t == PACK - 1),
                     is_transpose=True,
                 )
-            spent = sb.tile([P, P], F32, name=f"spent{b}_{qt}")
+
+        def row_sum(name, sums, denom, on_vector, slot):
+            spent = place([P, P], F32, name, slot)
             if on_vector:
-                nc.vector.tensor_scalar(
-                    spent[:], sums[:, 0, :], 4.0, 1.0, ALU.mult, ALU.add, accum_out=denom[:, qt : qt + 1]
-                )
+                nc.vector.tensor_scalar(spent[:], sums, 4.0, 1.0, ALU.mult, ALU.add, accum_out=denom)
             else:
-                nc.scalar.activation(
-                    spent[:], sums[:, 0, :], ACT.Copy, bias=1.0 / P, scale=4.0, accum_out=denom[:, qt : qt + 1]
-                )
+                nc.scalar.activation(spent[:], sums, ACT.Copy, bias=1.0 / P, scale=4.0, accum_out=denom)
 
         def invert(b, denom):
             inv = sb.tile([P, QT], F32, name=f"inv{b}")
@@ -227,13 +223,13 @@ def tile_attend_rel2_cap_kb_segb2q256n512t2048_kernel(tc, qT, k_words, k_scales,
             eng.tensor_tensor(
                 w_bf[:].rearrange("p (c i t) -> p c t i", i=4, t=PACK),
                 p4[:, :, qt * P : qt * P + width].rearrange("p t (c i) -> p c t i", i=4),
-                vs4[:, b, :].unsqueeze(1).unsqueeze(3).to_broadcast([P, width // 4, PACK, 4]),
+                vs4[:].unsqueeze(1).unsqueeze(3).to_broadcast([P, width // 4, PACK, 4]),
                 ALU.mult,
             )
             return w_bf
 
         def product(b, qt, w_codes, w_scales, v_codes, v_scales, inv, on_vector):
-            bank = mx.tile([P, 2, DV], F32, tag="mx", name="mxbank")
+            bank = ps.tile([P, 2, DV], F32, tag=f"mx{b}{qt}", name="y")
             nc.tensor.matmul_mx(
                 out=bank[:, 0, :],
                 lhsT=w_codes.bitcast(FP8X4),
@@ -248,45 +244,55 @@ def tile_attend_rel2_cap_kb_segb2q256n512t2048_kernel(tc, qT, k_words, k_scales,
                 nc.vector.tensor_scalar(res[:], bank[:, 0, :], inv[:, qt : qt + 1], None, ALU.mult)
             else:
                 nc.scalar.activation(res[:], bank[:, 0, :], ACT.Copy, scale=inv[:, qt : qt + 1])
-            nc.sync.dma_start(out[b, qt * P : (qt + 1) * P, :], res[:])
+            queue = nc.scalar if (b, qt) == (B - 1, QT - 1) else nc.sync
+            queue.dma_start(out[b, qt * P : (qt + 1) * P, :], res[:])
 
         den = [sb.tile([P, QT], F32, name=f"den{b}") for b in range(B)]
-        kb0 = bias_column(0, "kb_got0")
-        ks0 = key_scales(0, "ks_got0")
+        kb0 = token_column(kb_pool, "kb", 0, 0.5, "kb_got0", "kbcol")
+        ks0 = gather_scales(0, "ks_got0")
         q0 = cast_q(0, False)
         cast_v(0)
-        banks0 = scores(0, ks0, q0)
-        x0 = biased(0, banks0, kb0, ACT.Relu, "v_raw0")
-        kb1 = bias_column(1, "q_bf0")
-        ks1 = key_scales(1, "q0_codes")
         q1 = cast_q(1, False)
+        banks0 = scores(0, ks0, q0)
+        x0 = biased(0, banks0, kb0, ACT.Relu, 4608)
+        kb1 = token_column(kb_pool, "kb", 1, 0.5, "q_bf0", "kbcol")
+        ks1 = gather_scales(1, "q0_codes")
         banks1 = scores(1, ks1, q1)
-        t0 = sb.tile([P, PACK, NQ], F32, name="t0", tag="q_raw1", align_bytes=64)
-        nc.scalar.activation(flat(t0), flat(x0), ACT.Tanh)
+        t0 = place([P, PACK, NQ], F32, "t0", "t0")
+        halves = (slice(0, 2), slice(2, 4))
+        for h in halves:
+            nc.scalar.activation(t0[:, h, :], x0[:, h, :], ACT.Tanh)
+        p0 = place([P, PACK, NQ], F32, "p0", "p0")
+        for h in halves:
+            nc.scalar.activation(p0[:, h, :], t0[:, h, :], ACT.Square)
         cast_v(1)
-        p0 = sb.tile([P, PACK, NQ], F32, name="p0", tag="v_raw1", align_bytes=64)
-        nc.scalar.activation(flat(p0), flat(t0), ACT.Square)
         cast_v(2)
-        vs4 = token_columns(vs_pool, "vs", 4.0, "v_raw2")
+        vs0 = token_column(vs_pool, "vs", 0, 4.0, "q_bf1", 16384)
+        w0 = weights(0, p0, vs0, 0, NQ, nc.vector)
         cast_v(3)
-        t1 = biased(1, banks1, kb1, ACT.Tanh, "v_raw3")
-        vb0 = values(0)
-        w0 = weights(0, p0, vs4, 0, NQ, nc.vector)
-        vb1 = values(1)
-        v0 = values_out(0, vb0, "kbcol")
+        t1 = biased(1, banks1, kb1, ACT.Tanh, 16448)
+        vs1 = token_column(vs_pool, "vs", 1, 4.0, "keys0", "kbcol")
+        vb0 = values(0, "vals0")
+        vb1 = values(1, "vals1")
+        v0 = values_out(0, vb0, 20544)
+        sums0 = ps.tile([P, PACK, P], F32, tag="column0", name="sums0")
         for qt in range(QT):
-            row_sum(0, p0, qt, den[0], False)
+            turn_and_add(p0, qt, sums0[:, qt, :])
+        for qt in range(QT):
+            row_sum(f"spent0{qt}", sums0[:, qt, :], den[0][:, qt : qt + 1], False, 22592 + 512 * qt)
         v1 = values_out(1, vb1, "v_bf1")
-        w0_codes, w0_scales = quantize(w0[:], "w0")
         p1 = sb.tile([P, PACK, NQ], F32, name="p1")
         for qt in range(QT):
             cols = slice(qt * P, (qt + 1) * P)
             nc.vector.scalar_tensor_tensor(p1[:, :, cols], t1[:, :, cols], 0.0, t1[:, :, cols], ALU.max, ALU.mult)
+        w0_codes, w0_scales = quantize(w0[:], "w0", 23616)
         v0_codes, v0_scales = quantize(v0[:], "v0")
         inv0 = invert(0, den[0])
         for qt in range(QT):
-            row_sum(1, p1, qt, den[1], False)
-        w1 = [weights(1, p1, vs4, qt, P, nc.vector) for qt in range(QT)]
+            sums1 = ps.tile([P, PACK, P], F32, tag=("column1", "value0")[qt], name="sums1")
+            turn_and_add(p1, qt, sums1[:, 0, :])
+            row_sum(f"spent1{qt}", sums1[:, 0, :], den[1][:, qt : qt + 1], False, f"spent1{qt}")
+        w1 = [weights(1, p1, vs1, qt, P, nc.vector) for qt in range(QT)]
         for qt in range(QT):
             cols = slice(qt * P, (qt + 1) * P)
             product(0, qt, w0_codes[:, cols], w0_scales[:, cols], v0_codes, v0_scales, inv0, False)
@@ -294,4 +300,4 @@ def tile_attend_rel2_cap_kb_segb2q256n512t2048_kernel(tc, qT, k_words, k_scales,
         inv1 = invert(1, den[1])
         for qt in range(QT):
             codes, scales = quantize(w1[qt][:], f"w1_{qt}")
-            product(1, qt, codes[:], scales[:], v1_codes, v1_scales, inv1, qt == 1)
+            product(1, qt, codes[:], scales[:], v1_codes, v1_scales, inv1, qt == 0)

@@ -47,11 +47,11 @@ def tile_attend_rel2_cap_kb_segb2q256n512t2048_kernel(tc, qT, k_words, k_scales,
         warm = sb.tile([P, 1], F32, name="warm")
 
         nc.gpsimd.memset(ks_pool[:].bitcast(I32), 0)
-        nc.vector.memset(kb_pool[0:ROW, :], 0.0)
+        nc.vector.memset(kb_pool[0:ROW, :].bitcast(I32), 0)
+        nc.vector.memset(vs_pool[0:ROW, :].bitcast(I32), 0)
         nc.gpsimd.memset(warm[:], 0.0)
         nc.scalar.activation(warm[:], warm[:], ACT.Tanh)
         make_identity(nc, ident[:])
-        nc.gpsimd.memset(vs_pool[0:ROW, :], 0.0)
 
         nc.sync.dma_start(kb_pool[ROW:P, :], kb[0:1, :])
         words = k_words[0].rearrange("p t r -> p (t r)")
@@ -151,8 +151,7 @@ def tile_attend_rel2_cap_kb_segb2q256n512t2048_kernel(tc, qT, k_words, k_scales,
                 ACT.Copy,
             )
 
-        def scores(b, ks_got, q_bf):
-            keys = gather(kw_pool, b, "keys", I32, f"keys{b}")
+        def scores(b, keys, ks_got, q_bf):
             q_codes, q_scales = quantize(q_bf[:], f"q{b}")
             ks = deal_scales(b, ks_got)
             banks = []
@@ -249,15 +248,17 @@ def tile_attend_rel2_cap_kb_segb2q256n512t2048_kernel(tc, qT, k_words, k_scales,
 
         den = [sb.tile([P, QT], F32, name=f"den{b}") for b in range(B)]
         kb0 = token_column(kb_pool, "kb", 0, 0.5, "kb_got0", "kbcol")
+        keys0 = gather(kw_pool, 0, "keys", I32, "keys0")
         ks0 = gather_scales(0, "ks_got0")
         q0 = cast_q(0, False)
         cast_v(0)
         q1 = cast_q(1, False)
-        banks0 = scores(0, ks0, q0)
+        banks0 = scores(0, keys0, ks0, q0)
         x0 = biased(0, banks0, kb0, ACT.Relu, 4608)
         kb1 = token_column(kb_pool, "kb", 1, 0.5, "q_bf0", "kbcol")
         ks1 = gather_scales(1, "q0_codes")
-        banks1 = scores(1, ks1, q1)
+        keys1 = gather(kw_pool, 1, "keys", I32, "keys1")
+        banks1 = scores(1, keys1, ks1, q1)
         t0 = place([P, PACK, NQ], F32, "t0", "t0")
         halves = (slice(0, 2), slice(2, 4))
         for h in halves:

@@ -5,6 +5,7 @@ from concourse.masks import make_identity
 
 B, N, T, D, DV, NQ = 2, 512, 2048, 512, 256, 256
 FLOPS = 2 * B * NQ * N * (D + DV)
+BYTES = 4 * B * D * NQ + D * T + D // 32 * T + 4 * DV * T + 2 * 4 * T + 2 * 128 * 64 + 4 * B * NQ * DV
 
 F32 = mybir.dt.float32
 BF16 = mybir.dt.bfloat16
@@ -18,10 +19,25 @@ ACT = mybir.ActivationFunctionType
 
 P = 128
 PACK = 4
+RUN = 8
 SEG = T // B
-ROW = P - 1
+LIST_COLS = N // 16
 QT = NQ // P
-COLS = N // 16
+ROW = P - 1
+CHUNK = 512
+LINE = 4
+SCALAR_PLACES = 2
+
+RAW = 4096
+Q_AT = [RAW * b for b in range(B)]
+V_AT = [RAW * (B + c) for c in range(T // CHUNK)]
+COLUMN_AT = Q_AT[0] + N
+FIRST0_AT = Q_AT[1] + N
+VS0_AT = V_AT[2]
+FIRST1_AT = V_AT[2] + 64
+V0_AT = FIRST1_AT + RAW
+SPENT0_AT = V0_AT + 2 * DV * PACK
+W0_SCALES_AT = SPENT0_AT + QT * 4 * P
 
 
 def dealt(ap, run):
@@ -35,7 +51,12 @@ def tile_attend_rel2_cap_kb_segb2q256n512t2048_kernel(tc, qT, k_words, k_scales,
         stage = ctx.enter_context(tc.tile_pool(name="stage", bufs=1))
         ps = ctx.enter_context(tc.psum_pool(name="ps", bufs=1))
 
-        offsets = sb.tile([P, B * COLS], U16, name="offsets")
+        def place(shape, dtype, name, where):
+            if isinstance(where, int):
+                return stage.tile(shape, dtype, name=name, offset=where, align_bytes=64)
+            return sb.tile(shape, dtype, name=name, tag=where, align_bytes=64)
+
+        offsets = sb.tile([P, B * LIST_COLS], U16, name="offsets")
         nc.sync.dma_start(offsets[:], offs)
 
         ks_pool = sb.tile([P, T], U8, name="ks_pool", align_bytes=64)
@@ -44,38 +65,33 @@ def tile_attend_rel2_cap_kb_segb2q256n512t2048_kernel(tc, qT, k_words, k_scales,
         kw_pool = sb.tile([P, T], I32, name="kw_pool", align_bytes=64)
         v_pool = sb.tile([P, T], I32, name="v_pool", align_bytes=64)
         ident = sb.tile([P, P], F32, name="ident")
-        warm = sb.tile([P, 1], F32, name="warm")
+        zero = sb.tile([P, 1], F32, name="zero")
 
         nc.gpsimd.memset(ks_pool[:].bitcast(I32), 0)
         nc.vector.memset(kb_pool[0:ROW, :].bitcast(I32), 0)
         nc.vector.memset(vs_pool[0:ROW, :].bitcast(I32), 0)
-        nc.gpsimd.memset(warm[:], 0.0)
-        nc.scalar.activation(warm[:], warm[:], ACT.Tanh)
+        nc.gpsimd.memset(zero[:], 0.0)
+        nc.scalar.activation(zero[:], zero[:], ACT.Tanh)
         make_identity(nc, ident[:])
 
-        nc.sync.dma_start(kb_pool[ROW:P, :], kb[0:1, :])
-        words = k_words[0].rearrange("p t r -> p (t r)")
+        key_bytes = k_words[0].rearrange("p t r -> p (t r)")
         v_rows = vT.rearrange("(p h) t -> p h t", h=2)
-        q_raw = [stage.tile([P, PACK, NQ], F32, name=f"q_raw{b}", offset=4096 * b, align_bytes=64) for b in range(B)]
-        v_raw = [stage.tile([P, 2, 512], F32, name=f"v_raw{c}", offset=8192 + 4096 * c, align_bytes=64) for c in range(4)]
-
-        def place(shape, dtype, name, slot):
-            if isinstance(slot, int):
-                return stage.tile(shape, dtype, name=name, offset=slot, align_bytes=64)
-            return sb.tile(shape, dtype, name=name, tag=slot, align_bytes=64)
+        q_raw = [place([P, PACK, NQ], F32, f"q_raw{b}", Q_AT[b]) for b in range(B)]
+        v_raw = [place([P, 2, CHUNK], F32, f"v_raw{c}", V_AT[c]) for c in range(T // CHUNK)]
 
         def load_keys(b):
             nc.sync.dma_start(
                 kw_pool[:, b * SEG : (b + 1) * SEG],
-                words[:, b * SEG * PACK : (b + 1) * SEG * PACK].bitcast(I32),
+                key_bytes[:, b * SEG * PACK : (b + 1) * SEG * PACK].bitcast(I32),
             )
 
         def load_q(b):
             nc.sync.dma_start(q_raw[b][:], qT[b].rearrange("(p j) q -> p j q", j=PACK))
 
         def load_v(c):
-            nc.sync.dma_start(v_raw[c][:], v_rows[:, :, c * 512 : (c + 1) * 512])
+            nc.sync.dma_start(v_raw[c][:], v_rows[:, :, c * CHUNK : (c + 1) * CHUNK])
 
+        nc.sync.dma_start(kb_pool[ROW:P, :], kb[0:1, :])
         load_keys(0)
         for quad in range(4):
             nc.sync.dma_start(
@@ -87,83 +103,84 @@ def tile_attend_rel2_cap_kb_segb2q256n512t2048_kernel(tc, qT, k_words, k_scales,
         load_q(1)
         load_keys(1)
         nc.sync.dma_start(vs_pool[ROW:P, :], vs[0:1, :])
-        load_v(1)
-        load_v(2)
-        load_v(3)
+        for c in range(1, T // CHUNK):
+            load_v(c)
 
-        def gather(pool, b, name, dtype, slot):
-            got = place([P, N], dtype, f"{name}{b}", slot)
+        def list_of(b):
+            return offsets[:, b * LIST_COLS : (b + 1) * LIST_COLS]
+
+        def gather_words(pool, b, name):
+            got = sb.tile([P, N], I32, name=name, align_bytes=64)
             window = pool[:, 0 : (b + 1) * SEG].bitcast(U32)
-            nc.vector.tensor_copy(
-                dealt(got[:].bitcast(U32), 8), window.indirect(offsets[:, b * COLS : (b + 1) * COLS])
-            )
+            nc.vector.tensor_copy(dealt(got[:].bitcast(U32), RUN), window.indirect(list_of(b)))
             return got
 
-        def turn(src, tag):
-            bank = ps.tile([P, PACK, P], F32, tag=tag, name="turn")
-            for t in range(PACK):
-                nc.tensor.transpose(bank[:, t, :], src[:, t * P : (t + 1) * P].bitcast(F32), ident[:])
-            return bank
+        def gather_row(pool, name, where):
+            got = place([P, B * N], F32, name, where)
+            nc.vector.tensor_copy(dealt(got[:].bitcast(U32), RUN), pool[:].bitcast(U32).indirect(offsets[:]))
+            banks = []
+            for b in range(B):
+                bank = ps.tile([P, PACK, P], F32, tag=f"column{b}", name="turned_row")
+                for t in range(PACK):
+                    first = (t * B + b) * P
+                    nc.tensor.transpose(bank[:, t, :], got[:, first : first + P], ident[:])
+                banks.append(bank)
+            return banks
 
-        def token_column(pool, name, b, factor, got_slot, col_slot):
-            got = gather(pool, b, f"{name}_got", F32, got_slot)
-            bank = turn(got, f"column{b}")
-            col = place([P, PACK], F32, f"{name}col{b}", col_slot)
+        def column(bank, name, factor, where):
+            col = place([P, PACK], F32, name, where)
             nc.scalar.activation(col[:], bank[:, :, ROW], ACT.Copy, scale=factor)
             return col
 
-        def gather_scales(b, slot):
-            got = sb.tile([P, N], U8, name=f"ks_got{b}", tag=slot, align_bytes=64)
-            nc.vector.tensor_copy(
-                got[:], ks_pool[:, 0 : (b + 1) * SEG].indirect(offsets[:, b * COLS : (b + 1) * COLS])
-            )
+        def gather_scales(b, where):
+            got = place([P, N], U8, f"ks_got{b}", where)
+            nc.vector.tensor_copy(got[:], ks_pool[:, 0 : (b + 1) * SEG].indirect(list_of(b)))
             return got
 
         def deal_scales(b, got):
-            ks = place([P, N], U8, f"ks{b}", 4096 * b)
+            ks = place([P, N], U8, f"ks{b}", Q_AT[b])
             nc.vector.tensor_copy(
-                dealt(ks[:].bitcast(I32), 2),
-                got[:].bitcast(I32).rearrange("p (g t r) -> p g t r", t=PACK, r=2),
+                dealt(ks[:].bitcast(I32), RUN // 4),
+                got[:].bitcast(I32).rearrange("p (g t r) -> p g t r", t=PACK, r=RUN // 4),
             )
             return ks
 
-        def quantize(src, name, slot=None):
+        def quantize(src, name, scales_at):
             width = src.shape[1] // PACK
-            codes = sb.tile([P, width], U32, name=f"{name}_codes", tag=f"{name}_codes", align_bytes=64)
-            scales = place([P, width], U8, f"{name}_scales", slot or f"{name}_scales")
+            codes = sb.tile([P, width], U32, name=f"{name}_codes", align_bytes=64)
+            scales = place([P, width], U8, f"{name}_scales", scales_at)
             nc.vector.quantize_mx(out=codes[:].bitcast(FP8X4), scales=scales[:], in_=src)
             return codes, scales
 
-        def cast_q(b, on_pool):
-            q_bf = sb.tile([P, NQ * PACK], BF16, name=f"q_bf{b}", tag=f"q_bf{b}", align_bytes=64)
-            dst = q_bf[:].rearrange("p (c i j) -> p c j i", i=4, j=PACK)
-            src = q_raw[b][:].rearrange("p j (c i) -> p c j i", i=4)
-            if on_pool:
-                nc.gpsimd.tensor_scalar(dst, src, 1.0, 0.0, ALU.mult, ALU.add)
-            else:
-                nc.scalar.activation(dst, src, ACT.Copy)
+        def cast_q(b):
+            q_bf = place([P, NQ * PACK], BF16, f"q_bf{b}", f"q_bf{b}")
+            nc.scalar.activation(
+                q_bf[:].rearrange("p (c i j) -> p c j i", i=LINE, j=PACK),
+                q_raw[b][:].rearrange("p j (c i) -> p c j i", i=LINE),
+                ACT.Copy,
+            )
             return q_bf
 
         def cast_v(c):
             nc.scalar.activation(
-                v_pool[:, c * 512 : (c + 1) * 512].bitcast(BF16).rearrange("p (c h) -> p c h", h=2),
+                v_pool[:, c * CHUNK : (c + 1) * CHUNK].bitcast(BF16).rearrange("p (c h) -> p c h", h=2),
                 v_raw[c][:].rearrange("p h c -> p c h"),
                 ACT.Copy,
             )
 
         def scores(b, keys, ks_got, q_bf):
-            q_codes, q_scales = quantize(q_bf[:], f"q{b}")
+            q_codes, q_scales = quantize(q_bf[:], f"q{b}", f"q{b}_scales")
             ks = deal_scales(b, ks_got)
             banks = []
-            for u in range(2):
+            for u in range(PACK // 2):
                 bank = ps.tile([P, 2, NQ], F32, tag=f"mx{b}{u}", name="scores")
                 banks.append(bank)
                 for s in range(2):
-                    t = 2 * u + s
+                    cols = slice((2 * u + s) * P, (2 * u + s + 1) * P)
                     nc.tensor.matmul_mx(
                         out=bank[:, s, :],
-                        lhsT=keys[:, t * P : (t + 1) * P].bitcast(FP8X4),
-                        lhsT_scale=ks[:, t * P : (t + 1) * P],
+                        lhsT=keys[:, cols].bitcast(FP8X4),
+                        lhsT_scale=ks[:, cols],
                         rhs=q_codes[:].bitcast(FP8X4),
                         rhs_scale=q_scales[:],
                         start=True,
@@ -171,23 +188,27 @@ def tile_attend_rel2_cap_kb_segb2q256n512t2048_kernel(tc, qT, k_words, k_scales,
                     )
             return banks
 
-        def biased(b, banks, half_kb, func, slot):
-            first = place([P, PACK, NQ], F32, f"first{b}", slot)
+        def leave_psum(b, banks, half_kb, relu_places, where):
+            first = place([P, PACK, NQ], F32, f"first{b}", where)
             for t in range(PACK):
+                func = ACT.Relu if t < relu_places else ACT.Tanh
                 nc.scalar.activation(
                     first[:, t, :], banks[t // 2][:, t % 2, :], func, bias=half_kb[:, t : t + 1], scale=0.5
                 )
             return first
 
-        def flat(tile3):
-            return tile3[:].rearrange("p t q -> p (t q)")
+        def relu_square(dst, src):
+            nc.vector.scalar_tensor_tensor(dst, src, 0.0, src, ALU.max, ALU.mult)
 
-        def values(b, slot):
-            got = gather(v_pool, b, "vals", I32, slot)
-            return turn(got, f"value{b}")
+        def turn_values(b):
+            got = gather_words(v_pool, b, f"vals{b}")
+            bank = ps.tile([P, PACK, P], F32, tag=f"value{b}", name="turned_values")
+            for t in range(PACK):
+                nc.tensor.transpose(bank[:, t, :], got[:, t * P : (t + 1) * P].bitcast(F32), ident[:])
+            return bank
 
-        def values_out(b, bank, slot):
-            v_bf = place([P, DV * PACK], BF16, f"v_bf{b}", slot)
+        def interleave_values(b, bank, where):
+            v_bf = place([P, DV * PACK], BF16, f"v_bf{b}", where)
             nc.scalar.copy(
                 v_bf[:].rearrange("p (e t) -> p e t", t=PACK),
                 bank[:].rearrange("p t j -> p (t j)").bitcast(BF16).rearrange("p (t e) -> p e t", t=PACK),
@@ -205,29 +226,26 @@ def tile_attend_rel2_cap_kb_segb2q256n512t2048_kernel(tc, qT, k_words, k_scales,
                     is_transpose=True,
                 )
 
-        def row_sum(name, sums, denom, on_vector, slot):
-            spent = place([P, P], F32, name, slot)
-            if on_vector:
-                nc.vector.tensor_scalar(spent[:], sums, 4.0, 1.0, ALU.mult, ALU.add, accum_out=denom)
-            else:
-                nc.scalar.activation(spent[:], sums, ACT.Copy, bias=1.0 / P, scale=4.0, accum_out=denom)
+        def row_sum(sums, denom, name, where):
+            spent = place([P, P], F32, name, where)
+            nc.scalar.activation(spent[:], sums, ACT.Copy, bias=1.0 / P, scale=4.0, accum_out=denom)
 
         def invert(b, denom):
             inv = sb.tile([P, QT], F32, name=f"inv{b}")
             nc.vector.reciprocal(inv[:], denom[:])
             return inv
 
-        def weights(b, p4, vs4, qt, width, eng):
-            w_bf = sb.tile([P, width * PACK], BF16, name=f"w_bf{b}_{qt}", align_bytes=64)
-            eng.tensor_tensor(
-                w_bf[:].rearrange("p (c i t) -> p c t i", i=4, t=PACK),
-                p4[:, :, qt * P : qt * P + width].rearrange("p t (c i) -> p c t i", i=4),
-                vs4[:].unsqueeze(1).unsqueeze(3).to_broadcast([P, width // 4, PACK, 4]),
+        def weights(p4, vs4, first, width, name):
+            w_bf = sb.tile([P, width * PACK], BF16, name=name, align_bytes=64)
+            nc.vector.tensor_tensor(
+                w_bf[:].rearrange("p (c i t) -> p c t i", i=LINE, t=PACK),
+                p4[:, :, first : first + width].rearrange("p t (c i) -> p c t i", i=LINE),
+                vs4[:].unsqueeze(1).unsqueeze(3).to_broadcast([P, width // LINE, PACK, LINE]),
                 ALU.mult,
             )
             return w_bf
 
-        def product(b, qt, w_codes, w_scales, v_codes, v_scales, inv, on_vector):
+        def product(b, qt, w_codes, w_scales, v_codes, v_scales):
             bank = ps.tile([P, 2, DV], F32, tag=f"mx{b}{qt}", name="y")
             nc.tensor.matmul_mx(
                 out=bank[:, 0, :],
@@ -238,67 +256,78 @@ def tile_attend_rel2_cap_kb_segb2q256n512t2048_kernel(tc, qT, k_words, k_scales,
                 start=True,
                 stop=True,
             )
-            res = sb.tile([P, DV], F32, name=f"res{b}_{qt}")
-            if on_vector:
-                nc.vector.tensor_scalar(res[:], bank[:, 0, :], inv[:, qt : qt + 1], None, ALU.mult)
-            else:
-                nc.scalar.activation(res[:], bank[:, 0, :], ACT.Copy, scale=inv[:, qt : qt + 1])
-            queue = nc.scalar if (b, qt) == (B - 1, QT - 1) else nc.sync
+            return bank[:, 0, :]
+
+        def divide_on_scalar(b, qt, y, inv, queue):
+            res = sb.tile([P, DV], F32, name=f"res{b}{qt}")
+            nc.scalar.activation(res[:], y, ACT.Copy, scale=inv[:, qt : qt + 1])
             queue.dma_start(out[b, qt * P : (qt + 1) * P, :], res[:])
 
-        den = [sb.tile([P, QT], F32, name=f"den{b}") for b in range(B)]
-        kb0 = token_column(kb_pool, "kb", 0, 0.5, "kb_got0", "kbcol")
-        keys0 = gather(kw_pool, 0, "keys", I32, "keys0")
-        ks0 = gather_scales(0, "ks_got0")
-        q0 = cast_q(0, False)
+        def divide_on_vector(b, qt, y, inv):
+            res = sb.tile([P, DV], F32, name=f"res{b}{qt}")
+            nc.vector.tensor_scalar(res[:], y, inv[:, qt : qt + 1], None, ALU.mult)
+            nc.sync.dma_start(out[b, qt * P : (qt + 1) * P, :], res[:])
+
+        denom = [sb.tile([P, QT], F32, name=f"denom{b}") for b in range(B)]
+        q_tiles = [slice(qt * P, (qt + 1) * P) for qt in range(QT)]
+
+        kb_banks = gather_row(kb_pool, "kb_got", "kb_got")
+        keys0 = gather_words(kw_pool, 0, "keys0")
+        ks_got0 = gather_scales(0, "ks_got0")
+        q0 = cast_q(0)
+        half_kb0 = column(kb_banks[0], "half_kb0", 0.5, COLUMN_AT)
         cast_v(0)
-        q1 = cast_q(1, False)
-        banks0 = scores(0, keys0, ks0, q0)
-        x0 = biased(0, banks0, kb0, ACT.Relu, 4608)
-        kb1 = token_column(kb_pool, "kb", 1, 0.5, "q_bf0", "kbcol")
-        ks1 = gather_scales(1, "q0_codes")
-        keys1 = gather(kw_pool, 1, "keys", I32, "keys1")
-        banks1 = scores(1, keys1, ks1, q1)
-        t0 = place([P, PACK, NQ], F32, "t0", "t0")
-        halves = (slice(0, 2), slice(2, 4))
-        for h in halves:
-            nc.scalar.activation(t0[:, h, :], x0[:, h, :], ACT.Tanh)
-        p0 = place([P, PACK, NQ], F32, "p0", "p0")
-        for h in halves:
-            nc.scalar.activation(p0[:, h, :], t0[:, h, :], ACT.Square)
+        q1 = cast_q(1)
+        score_banks0 = scores(0, keys0, ks_got0, q0)
+        first0 = leave_psum(0, score_banks0, half_kb0, SCALAR_PLACES, FIRST0_AT)
+
+        ks_got1 = gather_scales(1, "q_bf0")
+        keys1 = gather_words(kw_pool, 1, "keys1")
+        score_banks1 = scores(1, keys1, ks_got1, q1)
+
+        capped0 = sb.tile([P, SCALAR_PLACES, NQ], F32, name="capped0")
+        p0 = sb.tile([P, PACK, NQ], F32, name="p0")
+        nc.scalar.activation(capped0[:], first0[:, 0:SCALAR_PLACES, :], ACT.Tanh, bias=zero[:])
+        half_kb1 = column(kb_banks[1], "half_kb1", 0.5, COLUMN_AT)
+        nc.scalar.activation(p0[:, 0:SCALAR_PLACES, :], capped0[:], ACT.Square)
         cast_v(1)
         cast_v(2)
-        vs0 = token_column(vs_pool, "vs", 0, 4.0, "q_bf1", 16384)
-        w0 = weights(0, p0, vs0, 0, NQ, nc.vector)
+        vs_banks = gather_row(vs_pool, "vs_got", "q_bf1")
+        relu_square(p0[:, SCALAR_PLACES:PACK, :], first0[:, SCALAR_PLACES:PACK, :])
+
+        vs4_0 = column(vs_banks[0], "vs4_0", 4.0, VS0_AT)
+        value_bank0 = turn_values(0)
+        w0 = weights(p0, vs4_0, 0, NQ, "w0")
         cast_v(3)
-        t1 = biased(1, banks1, kb1, ACT.Tanh, 16448)
-        vs1 = token_column(vs_pool, "vs", 1, 4.0, "keys0", "kbcol")
-        vb0 = values(0, "vals0")
-        vb1 = values(1, "vals1")
-        v0 = values_out(0, vb0, 20544)
+        capped1 = leave_psum(1, score_banks1, half_kb1, 0, FIRST1_AT)
+        vs4_1 = column(vs_banks[1], "vs4_1", 4.0, COLUMN_AT)
+        value_bank1 = turn_values(1)
+        v0 = interleave_values(0, value_bank0, V0_AT)
         sums0 = ps.tile([P, PACK, P], F32, tag="column0", name="sums0")
         for qt in range(QT):
             turn_and_add(p0, qt, sums0[:, qt, :])
         for qt in range(QT):
-            row_sum(f"spent0{qt}", sums0[:, qt, :], den[0][:, qt : qt + 1], False, 22592 + 512 * qt)
-        v1 = values_out(1, vb1, "v_bf1")
+            row_sum(sums0[:, qt, :], denom[0][:, qt : qt + 1], f"spent0{qt}", SPENT0_AT + 4 * P * qt)
+        v1 = interleave_values(1, value_bank1, "v_bf1")
+
         p1 = sb.tile([P, PACK, NQ], F32, name="p1")
-        for qt in range(QT):
-            cols = slice(qt * P, (qt + 1) * P)
-            nc.vector.scalar_tensor_tensor(p1[:, :, cols], t1[:, :, cols], 0.0, t1[:, :, cols], ALU.max, ALU.mult)
-        w0_codes, w0_scales = quantize(w0[:], "w0", 23616)
-        v0_codes, v0_scales = quantize(v0[:], "v0")
-        inv0 = invert(0, den[0])
-        for qt in range(QT):
-            sums1 = ps.tile([P, PACK, P], F32, tag=("column1", "value0")[qt], name="sums1")
+        for cols in q_tiles:
+            relu_square(p1[:, :, cols], capped1[:, :, cols])
+        w0_codes, w0_scales = quantize(w0[:], "w0", W0_SCALES_AT)
+        v0_codes, v0_scales = quantize(v0[:], "v0", "v0_scales")
+        inv0 = invert(0, denom[0])
+        for qt, tag in enumerate(("column1", "value0")):
+            sums1 = ps.tile([P, PACK, P], F32, tag=tag, name="sums1")
             turn_and_add(p1, qt, sums1[:, 0, :])
-            row_sum(f"spent1{qt}", sums1[:, 0, :], den[1][:, qt : qt + 1], False, f"spent1{qt}")
-        w1 = [weights(1, p1, vs1, qt, P, nc.vector) for qt in range(QT)]
-        for qt in range(QT):
-            cols = slice(qt * P, (qt + 1) * P)
-            product(0, qt, w0_codes[:, cols], w0_scales[:, cols], v0_codes, v0_scales, inv0, False)
-        v1_codes, v1_scales = quantize(v1[:], "v1")
-        inv1 = invert(1, den[1])
-        for qt in range(QT):
-            codes, scales = quantize(w1[qt][:], f"w1_{qt}")
-            product(1, qt, codes[:], scales[:], v1_codes, v1_scales, inv1, qt == 0)
+            row_sum(sums1[:, 0, :], denom[1][:, qt : qt + 1], f"spent1{qt}", f"spent1{qt}")
+        w1 = [weights(p1, vs4_1, qt * P, P, f"w1{qt}") for qt in range(QT)]
+
+        for qt, cols in enumerate(q_tiles):
+            y = product(0, qt, w0_codes[:, cols], w0_scales[:, cols], v0_codes, v0_scales)
+            divide_on_scalar(0, qt, y, inv0, nc.sync)
+        v1_codes, v1_scales = quantize(v1[:], "v1", "v1_scales")
+        inv1 = invert(1, denom[1])
+        codes, scales = quantize(w1[0][:], "w10", "w10_scales")
+        divide_on_vector(1, 0, product(1, 0, codes[:], scales[:], v1_codes, v1_scales), inv1)
+        codes, scales = quantize(w1[1][:], "w11", "w11_scales")
+        divide_on_scalar(1, 1, product(1, 1, codes[:], scales[:], v1_codes, v1_scales), inv1, nc.scalar)

from contextlib import ExitStack

import concourse.mybir as mybir
from concourse.masks import make_identity

B, N, T, D, DV, NQ = 2, 512, 2048, 512, 256, 256
FLOPS = 2 * B * NQ * N * (D + DV)
BYTES = 4 * B * D * NQ + D * T + D // 32 * T + 4 * DV * T + 2 * 4 * T + 2 * 128 * 64 + 4 * B * NQ * DV

F32 = mybir.dt.float32
BF16 = mybir.dt.bfloat16
I32 = mybir.dt.int32
U32 = mybir.dt.uint32
U16 = mybir.dt.uint16
U8 = mybir.dt.uint8
FP8X4 = mybir.dt.float8_e4m3fn_x4
ALU = mybir.AluOpType
ACT = mybir.ActivationFunctionType

P = 128
PACK = 4
RUN = 8
SEG = T // B
LIST_COLS = N // 16
QT = NQ // P
ROW = P - 1
CHUNK = 512
LINE = 4
SCALAR_PLACES = 2

RAW = 4096
Q_AT = [RAW * b for b in range(B)]
V_AT = [RAW * (B + c) for c in range(T // CHUNK)]
COLUMN_AT = Q_AT[0] + N
FIRST0_AT = Q_AT[1] + N
VS0_AT = V_AT[2]
FIRST1_AT = V_AT[2] + 64
V0_AT = FIRST1_AT + RAW
SPENT0_AT = V0_AT + 2 * DV * PACK
W0_SCALES_AT = SPENT0_AT + QT * 4 * P


def dealt(ap, run):
    return ap.rearrange("p (t g r) -> p g t r", t=PACK, r=run)


def tile_attend_rel2_cap_kb_segb2q256n512t2048_kernel(tc, qT, k_words, k_scales, vT, vs, kb, offs, out):
    nc = tc.nc
    with ExitStack() as ctx:
        sb = ctx.enter_context(tc.tile_pool(name="sb", bufs=1))
        stage = ctx.enter_context(tc.tile_pool(name="stage", bufs=1))
        ps = ctx.enter_context(tc.psum_pool(name="ps", bufs=1))

        def place(shape, dtype, name, where):
            if isinstance(where, int):
                return stage.tile(shape, dtype, name=name, offset=where, align_bytes=64)
            return sb.tile(shape, dtype, name=name, tag=where, align_bytes=64)

        offsets = sb.tile([P, B * LIST_COLS], U16, name="offsets")
        nc.sync.dma_start(offsets[:], offs)

        ks_pool = sb.tile([P, T], U8, name="ks_pool", align_bytes=64)
        kb_pool = sb.tile([P, T], F32, name="kb_pool", align_bytes=64)
        vs_pool = sb.tile([P, T], F32, name="vs_pool", align_bytes=64)
        kw_pool = sb.tile([P, T], I32, name="kw_pool", align_bytes=64)
        v_pool = sb.tile([P, T], I32, name="v_pool", align_bytes=64)
        ident = sb.tile([P, P], F32, name="ident")
        zero = sb.tile([P, 1], F32, name="zero")

        nc.gpsimd.memset(ks_pool[:].bitcast(I32), 0)
        nc.vector.memset(kb_pool[0:ROW, :].bitcast(I32), 0)
        nc.vector.memset(vs_pool[0:ROW, :].bitcast(I32), 0)
        nc.gpsimd.memset(zero[:], 0.0)
        nc.scalar.activation(zero[:], zero[:], ACT.Tanh)
        make_identity(nc, ident[:])

        key_bytes = k_words[0].rearrange("p t r -> p (t r)")
        v_rows = vT.rearrange("(p h) t -> p h t", h=2)
        q_raw = [place([P, PACK, NQ], F32, f"q_raw{b}", Q_AT[b]) for b in range(B)]
        v_raw = [place([P, 2, CHUNK], F32, f"v_raw{c}", V_AT[c]) for c in range(T // CHUNK)]

        def load_keys(b):
            nc.sync.dma_start(
                kw_pool[:, b * SEG : (b + 1) * SEG],
                key_bytes[:, b * SEG * PACK : (b + 1) * SEG * PACK].bitcast(I32),
            )

        def load_q(b):
            nc.sync.dma_start(q_raw[b][:], qT[b].rearrange("(p j) q -> p j q", j=PACK))

        def load_v(c):
            nc.sync.dma_start(v_raw[c][:], v_rows[:, :, c * CHUNK : (c + 1) * CHUNK])

        nc.sync.dma_start(kb_pool[ROW:P, :], kb[0:1, :])
        load_keys(0)
        for quad in range(4):
            nc.sync.dma_start(
                ks_pool[32 * quad : 32 * quad + 4, :].bitcast(I32),
                k_scales[0, 4 * quad : 4 * quad + 4, :].bitcast(I32),
            )
        load_q(0)
        load_v(0)
        load_q(1)
        load_keys(1)
        nc.sync.dma_start(vs_pool[ROW:P, :], vs[0:1, :])
        for c in range(1, T // CHUNK):
            load_v(c)

        def list_of(b):
            return offsets[:, b * LIST_COLS : (b + 1) * LIST_COLS]

        def gather_words(pool, b, name):
            got = sb.tile([P, N], I32, name=name, align_bytes=64)
            window = pool[:, 0 : (b + 1) * SEG].bitcast(U32)
            nc.vector.tensor_copy(dealt(got[:].bitcast(U32), RUN), window.indirect(list_of(b)))
            return got

        def gather_row(pool, name, where):
            got = place([P, B * N], F32, name, where)
            nc.vector.tensor_copy(dealt(got[:].bitcast(U32), RUN), pool[:].bitcast(U32).indirect(offsets[:]))
            banks = []
            for b in range(B):
                bank = ps.tile([P, PACK, P], F32, tag=f"column{b}", name="turned_row")
                for t in range(PACK):
                    first = (t * B + b) * P
                    nc.tensor.transpose(bank[:, t, :], got[:, first : first + P], ident[:])
                banks.append(bank)
            return banks

        def column(bank, name, factor, where):
            col = place([P, PACK], F32, name, where)
            nc.scalar.activation(col[:], bank[:, :, ROW], ACT.Copy, scale=factor)
            return col

        def gather_scales(b, where):
            got = place([P, N], U8, f"ks_got{b}", where)
            nc.vector.tensor_copy(got[:], ks_pool[:, 0 : (b + 1) * SEG].indirect(list_of(b)))
            return got

        def deal_scales(b, got):
            ks = place([P, N], U8, f"ks{b}", Q_AT[b])
            nc.vector.tensor_copy(
                dealt(ks[:].bitcast(I32), RUN // 4),
                got[:].bitcast(I32).rearrange("p (g t r) -> p g t r", t=PACK, r=RUN // 4),
            )
            return ks

        def quantize(src, name, scales_at):
            width = src.shape[1] // PACK
            codes = sb.tile([P, width], U32, name=f"{name}_codes", align_bytes=64)
            scales = place([P, width], U8, f"{name}_scales", scales_at)
            nc.vector.quantize_mx(out=codes[:].bitcast(FP8X4), scales=scales[:], in_=src)
            return codes, scales

        def cast_q(b):
            q_bf = place([P, NQ * PACK], BF16, f"q_bf{b}", f"q_bf{b}")
            nc.scalar.activation(
                q_bf[:].rearrange("p (c i j) -> p c j i", i=LINE, j=PACK),
                q_raw[b][:].rearrange("p j (c i) -> p c j i", i=LINE),
                ACT.Copy,
            )
            return q_bf

        def cast_v(c):
            nc.scalar.activation(
                v_pool[:, c * CHUNK : (c + 1) * CHUNK].bitcast(BF16).rearrange("p (c h) -> p c h", h=2),
                v_raw[c][:].rearrange("p h c -> p c h"),
                ACT.Copy,
            )

        def scores(b, keys, ks_got, q_bf):
            q_codes, q_scales = quantize(q_bf[:], f"q{b}", f"q{b}_scales")
            ks = deal_scales(b, ks_got)
            banks = []
            for u in range(PACK // 2):
                bank = ps.tile([P, 2, NQ], F32, tag=f"mx{b}{u}", name="scores")
                banks.append(bank)
                for s in range(2):
                    cols = slice((2 * u + s) * P, (2 * u + s + 1) * P)
                    nc.tensor.matmul_mx(
                        out=bank[:, s, :],
                        lhsT=keys[:, cols].bitcast(FP8X4),
                        lhsT_scale=ks[:, cols],
                        rhs=q_codes[:].bitcast(FP8X4),
                        rhs_scale=q_scales[:],
                        start=True,
                        stop=True,
                    )
            return banks

        def leave_psum(b, banks, half_kb, relu_places, where):
            first = place([P, PACK, NQ], F32, f"first{b}", where)
            for t in range(PACK):
                func = ACT.Relu if t < relu_places else ACT.Tanh
                nc.scalar.activation(
                    first[:, t, :], banks[t // 2][:, t % 2, :], func, bias=half_kb[:, t : t + 1], scale=0.5
                )
            return first

        def relu_square(dst, src):
            nc.vector.scalar_tensor_tensor(dst, src, 0.0, src, ALU.max, ALU.mult)

        def turn_values(b):
            got = gather_words(v_pool, b, f"vals{b}")
            bank = ps.tile([P, PACK, P], F32, tag=f"value{b}", name="turned_values")
            for t in range(PACK):
                nc.tensor.transpose(bank[:, t, :], got[:, t * P : (t + 1) * P].bitcast(F32), ident[:])
            return bank

        def interleave_values(b, bank, where):
            v_bf = place([P, DV * PACK], BF16, f"v_bf{b}", where)
            nc.scalar.copy(
                v_bf[:].rearrange("p (e t) -> p e t", t=PACK),
                bank[:].rearrange("p t j -> p (t j)").bitcast(BF16).rearrange("p (t e) -> p e t", t=PACK),
            )
            return v_bf

        def turn_and_add(p4, qt, dst):
            for t in range(PACK):
                nc.tensor.matmul(
                    dst,
                    p4[:, t, qt * P : (qt + 1) * P],
                    ident[:],
                    start=(t == 0),
                    stop=(t == PACK - 1),
                    is_transpose=True,
                )

        def row_sum(sums, denom, name, where):
            spent = place([P, P], F32, name, where)
            nc.scalar.activation(spent[:], sums, ACT.Copy, bias=1.0 / P, scale=4.0, accum_out=denom)

        def invert(b, denom):
            inv = sb.tile([P, QT], F32, name=f"inv{b}")
            nc.vector.reciprocal(inv[:], denom[:])
            return inv

        def weights(p4, vs4, first, width, name):
            w_bf = sb.tile([P, width * PACK], BF16, name=name, align_bytes=64)
            nc.vector.tensor_tensor(
                w_bf[:].rearrange("p (c i t) -> p c t i", i=LINE, t=PACK),
                p4[:, :, first : first + width].rearrange("p t (c i) -> p c t i", i=LINE),
                vs4[:].unsqueeze(1).unsqueeze(3).to_broadcast([P, width // LINE, PACK, LINE]),
                ALU.mult,
            )
            return w_bf

        def product(b, qt, w_codes, w_scales, v_codes, v_scales):
            bank = ps.tile([P, 2, DV], F32, tag=f"mx{b}{qt}", name="y")
            nc.tensor.matmul_mx(
                out=bank[:, 0, :],
                lhsT=w_codes.bitcast(FP8X4),
                lhsT_scale=w_scales,
                rhs=v_codes[:].bitcast(FP8X4),
                rhs_scale=v_scales[:],
                start=True,
                stop=True,
            )
            return bank[:, 0, :]

        def divide_on_scalar(b, qt, y, inv, queue):
            res = sb.tile([P, DV], F32, name=f"res{b}{qt}")
            nc.scalar.activation(res[:], y, ACT.Copy, scale=inv[:, qt : qt + 1])
            queue.dma_start(out[b, qt * P : (qt + 1) * P, :], res[:])

        def divide_on_vector(b, qt, y, inv):
            res = sb.tile([P, DV], F32, name=f"res{b}{qt}")
            nc.vector.tensor_scalar(res[:], y, inv[:, qt : qt + 1], None, ALU.mult)
            nc.sync.dma_start(out[b, qt * P : (qt + 1) * P, :], res[:])

        denom = [sb.tile([P, QT], F32, name=f"denom{b}") for b in range(B)]
        q_tiles = [slice(qt * P, (qt + 1) * P) for qt in range(QT)]

        kb_banks = gather_row(kb_pool, "kb_got", "kb_got")
        keys0 = gather_words(kw_pool, 0, "keys0")
        ks_got0 = gather_scales(0, "ks_got0")
        q0 = cast_q(0)
        half_kb0 = column(kb_banks[0], "half_kb0", 0.5, COLUMN_AT)
        cast_v(0)
        q1 = cast_q(1)
        score_banks0 = scores(0, keys0, ks_got0, q0)
        first0 = leave_psum(0, score_banks0, half_kb0, SCALAR_PLACES, FIRST0_AT)

        ks_got1 = gather_scales(1, "q_bf0")
        keys1 = gather_words(kw_pool, 1, "keys1")
        score_banks1 = scores(1, keys1, ks_got1, q1)

        capped0 = sb.tile([P, SCALAR_PLACES, NQ], F32, name="capped0")
        p0 = sb.tile([P, PACK, NQ], F32, name="p0")
        nc.scalar.activation(capped0[:], first0[:, 0:SCALAR_PLACES, :], ACT.Tanh, bias=zero[:])
        half_kb1 = column(kb_banks[1], "half_kb1", 0.5, COLUMN_AT)
        nc.scalar.activation(p0[:, 0:SCALAR_PLACES, :], capped0[:], ACT.Square)
        cast_v(1)
        cast_v(2)
        vs_banks = gather_row(vs_pool, "vs_got", "q_bf1")
        relu_square(p0[:, SCALAR_PLACES:PACK, :], first0[:, SCALAR_PLACES:PACK, :])

        vs4_0 = column(vs_banks[0], "vs4_0", 4.0, VS0_AT)
        value_bank0 = turn_values(0)
        w0 = weights(p0, vs4_0, 0, NQ, "w0")
        cast_v(3)
        capped1 = leave_psum(1, score_banks1, half_kb1, 0, FIRST1_AT)
        vs4_1 = column(vs_banks[1], "vs4_1", 4.0, COLUMN_AT)
        value_bank1 = turn_values(1)
        v0 = interleave_values(0, value_bank0, V0_AT)
        sums0 = ps.tile([P, PACK, P], F32, tag="column0", name="sums0")
        for qt in range(QT):
            turn_and_add(p0, qt, sums0[:, qt, :])
        for qt in range(QT):
            row_sum(sums0[:, qt, :], denom[0][:, qt : qt + 1], f"spent0{qt}", SPENT0_AT + 4 * P * qt)
        v1 = interleave_values(1, value_bank1, "v_bf1")

        p1 = sb.tile([P, PACK, NQ], F32, name="p1")
        for cols in q_tiles:
            relu_square(p1[:, :, cols], capped1[:, :, cols])
        w0_codes, w0_scales = quantize(w0[:], "w0", W0_SCALES_AT)
        v0_codes, v0_scales = quantize(v0[:], "v0", "v0_scales")
        inv0 = invert(0, denom[0])
        for qt, tag in enumerate(("column1", "value0")):
            sums1 = ps.tile([P, PACK, P], F32, tag=tag, name="sums1")
            turn_and_add(p1, qt, sums1[:, 0, :])
            row_sum(sums1[:, 0, :], denom[1][:, qt : qt + 1], f"spent1{qt}", f"spent1{qt}")
        w1 = [weights(p1, vs4_1, qt * P, P, f"w1{qt}") for qt in range(QT)]

        for qt, cols in enumerate(q_tiles):
            y = product(0, qt, w0_codes[:, cols], w0_scales[:, cols], v0_codes, v0_scales)
            divide_on_scalar(0, qt, y, inv0, nc.sync)
        v1_codes, v1_scales = quantize(v1[:], "v1", "v1_scales")
        inv1 = invert(1, denom[1])
        codes, scales = quantize(w1[0][:], "w10", "w10_scales")
        divide_on_vector(1, 0, product(1, 0, codes[:], scales[:], v1_codes, v1_scales), inv1)
        codes, scales = quantize(w1[1][:], "w11", "w11_scales")
        divide_on_scalar(1, 1, product(1, 1, codes[:], scales[:], v1_codes, v1_scales), inv1, nc.scalar)
